import numpy as np
CORES = [72,73,74,75,76,77,78,79,456,457,458,459,460,461,462,463]
N = 16
def setup_inputs(rng):
    return {"x": rng.standard_normal((N, 128, 512), dtype=np.float32)}
def reference(x):
    s = x.sum(axis=0, dtype=np.float64).astype(x.dtype)
    return {"y": np.broadcast_to(s, (N,) + s.shape)}

@@ -1,0 +1,55 @@
+from concourse.bass import DstId, RemoteDMATransfer
+from concourse.mybir import AluOpType
+NB = 8
+NCH = 2
+W = 512 // (NB * NCH)
+RC = 128 // NCH
+SCRATCH = {'xs': ('dram', [NCH * NB, 128, W], 'float32'), 'land': ('dram', [NCH * NB, 128, W], 'float32'), 'pa': ('dram', [NCH, 128, W], 'float32'), 'pb': ('dram', [NCH, 128, W], 'float32'), 'out': ('dram', [NCH * NB, 128, W], 'float32')}
+SEMAPHORES = ['stored', 'read'] + ['loaded%d' % c for c in range(NCH)] + ['added%d' % c for c in range(NCH)] + ['arr1_%d' % c for c in range(NCH)] + ['arr2_%d' % c for c in range(NCH)] + ['arr3_%d' % c for c in range(NCH)]
+
+def rank_program(g, core, T, topo):
+    rank = T.rank_of(core)
+    if rank is None:
+        return
+    i = core % 8
+    n = i ^ 1
+    base = core - i
+    other = [c for c in T.cores if c - c % 8 != base][0]
+    obase = other - other % 8
+    S = T.sem
+    loaded = [S.loaded0, S.loaded1][:NCH]
+    added = [S.added0, S.added1][:NCH]
+    arr1 = [S.arr1_0, S.arr1_1][:NCH]
+    arr2 = [S.arr2_0, S.arr2_1][:NCH]
+    arr3 = [S.arr3_0, S.arr3_1][:NCH]
+
+    def did(dst):
+        rid, pid = topo.addr(dst, core)
+        return DstId(rid=rid, pnc=pid)
+    for c in range(NCH):
+        g.dma_start(T.xs[c * NB:(c + 1) * NB], T.x[c * RC:(c + 1) * RC, :]).then_inc(loaded[c], 16)
+    for c in range(NCH):
+        g.wait_ge(loaded[c], 16)
+        trs = []
+        k = 0
+        for b in range(NB):
+            if b == i:
+                continue
+            trs.append(RemoteDMATransfer(dst_ids=[did(base + b)], dma_engine_mask=3 << 2 * k, remote_sem=arr1[c], src=T.xs[c * NB + b], dst=T.land[c * NB + i]))
+            k += 1
+        g.remote_dma_fused(trs, local_sem=S.read)
+    for c in range(NCH):
+        g.wait_ge(arr1[c], 14)
+        srcs = [T.xs[c * NB + i] if j == i else T.land[c * NB + j] for j in range(NB)]
+        g.remote_dma_fused([RemoteDMATransfer(dst_ids=[did(obase + n)], dma_engine_mask=255, remote_sem=arr2[c], srcs=srcs, dsts=[T.pb[c]], alu_op=1), RemoteDMATransfer(dst_ids=[did(base + n), did(base + n)], dma_engine_mask=65280, remote_sem=arr2[c], srcs=srcs, dsts=[T.pa[c], T.out[c * NB + i]], alu_op=1)], local_sem=S.read)
+    others = [base + j for j in range(NB) if j != i]
+    for c in range(NCH):
+        g.wait_ge(arr2[c], 24)
+        g.remote_dma_fused([RemoteDMATransfer(dst_ids=[did(d) for d in others], dma_engine_mask=65535, remote_sem=arr3[c], srcs=[T.pa[c], T.pb[c]], dsts=[T.out[c * NB + n] for d in others], alu_op=1)], local_sem=S.read)
+        g.dma_start(T.out[c * NB + n], T.pb[c], accum_op=AluOpType.add, max_dma_last_dim=8192).then_inc(added[c], 16)
+    for c in range(NCH):
+        g.wait_ge(arr3[c], 7 * 16)
+        g.wait_ge(added[c], 16)
+        g.dma_start(T.y[c * RC:(c + 1) * RC, :], T.out[c * NB:(c + 1) * NB]).then_inc(S.stored, 16)
+    g.wait_ge(S.read, NCH * (14 + 16 + 16))
+    g.wait_ge(S.stored, NCH * 16)

@@ -7,6 +7,7 @@ RC = 128 // NCH
 SCRATCH = {'xs': ('dram', [NCH * NB, 128, W], 'float32'), 'land': ('dram', [NCH * NB, 128, W], 'float32'), 'pa': ('dram', [NCH, 128, W], 'float32'), 'pb': ('dram', [NCH, 128, W], 'float32'), 'out': ('dram', [NCH * NB, 128, W], 'float32')}
 SEMAPHORES = ['stored', 'read'] + ['loaded%d' % c for c in range(NCH)] + ['added%d' % c for c in range(NCH)] + ['arr1_%d' % c for c in range(NCH)] + ['arr2_%d' % c for c in range(NCH)] + ['arr3_%d' % c for c in range(NCH)]
 
+
 def rank_program(g, core, T, topo):
     rank = T.rank_of(core)
     if rank is None:
@@ -22,12 +23,13 @@ def rank_program(g, core, T, topo):
     arr1 = [S.arr1_0, S.arr1_1][:NCH]
     arr2 = [S.arr2_0, S.arr2_1][:NCH]
     arr3 = [S.arr3_0, S.arr3_1][:NCH]
+    hw = [g.sync, g.scalar]
 
     def did(dst):
         rid, pid = topo.addr(dst, core)
         return DstId(rid=rid, pnc=pid)
     for c in range(NCH):
-        g.dma_start(T.xs[c * NB:(c + 1) * NB], T.x[c * RC:(c + 1) * RC, :]).then_inc(loaded[c], 16)
+        hw[c % 2].dma_start(T.xs[c * NB:(c + 1) * NB], T.x[c * RC:(c + 1) * RC, :]).then_inc(loaded[c], 16)
     for c in range(NCH):
         g.wait_ge(loaded[c], 16)
         trs = []
@@ -48,8 +50,9 @@ def rank_program(g, core, T, topo):
         g.remote_dma_fused([RemoteDMATransfer(dst_ids=[did(d) for d in others], dma_engine_mask=65535, remote_sem=arr3[c], srcs=[T.pa[c], T.pb[c]], dsts=[T.out[c * NB + n] for d in others], alu_op=1)], local_sem=S.read)
         g.dma_start(T.out[c * NB + n], T.pb[c], accum_op=AluOpType.add, max_dma_last_dim=8192).then_inc(added[c], 16)
     for c in range(NCH):
-        g.wait_ge(arr3[c], 7 * 16)
-        g.wait_ge(added[c], 16)
-        g.dma_start(T.y[c * RC:(c + 1) * RC, :], T.out[c * NB:(c + 1) * NB]).then_inc(S.stored, 16)
+        q = hw[c % 2]
+        q.wait_ge(arr3[c], 7 * 16)
+        q.wait_ge(added[c], 16)
+        q.dma_start(T.y[c * RC:(c + 1) * RC, :], T.out[c * NB:(c + 1) * NB]).then_inc(S.stored, 16)
     g.wait_ge(S.read, NCH * (14 + 16 + 16))
     g.wait_ge(S.stored, NCH * 16)

from concourse.bass import DstId, RemoteDMATransfer
from concourse.mybir import AluOpType
NB = 8
NCH = 2
W = 512 // (NB * NCH)
RC = 128 // NCH
SCRATCH = {'xs': ('dram', [NCH * NB, 128, W], 'float32'), 'land': ('dram', [NCH * NB, 128, W], 'float32'), 'pa': ('dram', [NCH, 128, W], 'float32'), 'pb': ('dram', [NCH, 128, W], 'float32'), 'out': ('dram', [NCH * NB, 128, W], 'float32')}
SEMAPHORES = ['stored', 'read'] + ['loaded%d' % c for c in range(NCH)] + ['added%d' % c for c in range(NCH)] + ['arr1_%d' % c for c in range(NCH)] + ['arr2_%d' % c for c in range(NCH)] + ['arr3_%d' % c for c in range(NCH)]


def rank_program(g, core, T, topo):
    rank = T.rank_of(core)
    if rank is None:
        return
    i = core % 8
    n = i ^ 1
    base = core - i
    other = [c for c in T.cores if c - c % 8 != base][0]
    obase = other - other % 8
    S = T.sem
    loaded = [S.loaded0, S.loaded1][:NCH]
    added = [S.added0, S.added1][:NCH]
    arr1 = [S.arr1_0, S.arr1_1][:NCH]
    arr2 = [S.arr2_0, S.arr2_1][:NCH]
    arr3 = [S.arr3_0, S.arr3_1][:NCH]
    hw = [g.sync, g.scalar]

    def did(dst):
        rid, pid = topo.addr(dst, core)
        return DstId(rid=rid, pnc=pid)
    for c in range(NCH):
        hw[c % 2].dma_start(T.xs[c * NB:(c + 1) * NB], T.x[c * RC:(c + 1) * RC, :]).then_inc(loaded[c], 16)
    for c in range(NCH):
        g.wait_ge(loaded[c], 16)
        trs = []
        k = 0
        for b in range(NB):
            if b == i:
                continue
            trs.append(RemoteDMATransfer(dst_ids=[did(base + b)], dma_engine_mask=3 << 2 * k, remote_sem=arr1[c], src=T.xs[c * NB + b], dst=T.land[c * NB + i]))
            k += 1
        g.remote_dma_fused(trs, local_sem=S.read)
    for c in range(NCH):
        g.wait_ge(arr1[c], 14)
        srcs = [T.xs[c * NB + i] if j == i else T.land[c * NB + j] for j in range(NB)]
        g.remote_dma_fused([RemoteDMATransfer(dst_ids=[did(obase + n)], dma_engine_mask=255, remote_sem=arr2[c], srcs=srcs, dsts=[T.pb[c]], alu_op=1), RemoteDMATransfer(dst_ids=[did(base + n), did(base + n)], dma_engine_mask=65280, remote_sem=arr2[c], srcs=srcs, dsts=[T.pa[c], T.out[c * NB + i]], alu_op=1)], local_sem=S.read)
    others = [base + j for j in range(NB) if j != i]
    for c in range(NCH):
        g.wait_ge(arr2[c], 24)
        g.remote_dma_fused([RemoteDMATransfer(dst_ids=[did(d) for d in others], dma_engine_mask=65535, remote_sem=arr3[c], srcs=[T.pa[c], T.pb[c]], dsts=[T.out[c * NB + n] for d in others], alu_op=1)], local_sem=S.read)
        g.dma_start(T.out[c * NB + n], T.pb[c], accum_op=AluOpType.add, max_dma_last_dim=8192).then_inc(added[c], 16)
    for c in range(NCH):
        q = hw[c % 2]
        q.wait_ge(arr3[c], 7 * 16)
        q.wait_ge(added[c], 16)
        q.dma_start(T.y[c * RC:(c + 1) * RC, :], T.out[c * NB:(c + 1) * NB]).then_inc(S.stored, 16)
    g.wait_ge(S.read, NCH * (14 + 16 + 16))
    g.wait_ge(S.stored, NCH * 16)
